import numpy as np
import ml_dtypes


def mxq(x, axis, fmt="e4m3"):
    dtype, down = {"e4m3": (ml_dtypes.float8_e4m3fn, 7), "e5m2": (ml_dtypes.float8_e5m2, 14)}[fmt]
    v = np.moveaxis(np.asarray(x, np.float32).astype(ml_dtypes.bfloat16).astype(np.float64), axis, -1)
    blocks = v.reshape(v.shape[:-1] + (-1, 32))
    amax = np.abs(blocks).max(-1, keepdims=True)
    byte = np.maximum(np.where(amax > 0, np.frexp(amax)[1] - 1 + 127, 0) - down, 1)
    scale = np.exp2(byte - 127.0)
    codes = (blocks / scale).astype(np.float32).astype(dtype).astype(np.float64)
    return np.moveaxis((codes * scale).reshape(v.shape), -1, axis)


WIDE = False


def mx_kscale(k):
    if not WIDE:
        return np.ones(k)
    levels = np.array([10, -10, 5, -5, 0])
    if k % 512:
        return np.exp2(np.random.permutation(np.resize(levels, k // 32))).repeat(32)
    a = np.empty((k // 512, 16))
    for p in range(k // 512):
        a[p, :8] = np.random.permutation(np.resize(levels, 8))
        for g in range(8):
            far = levels[np.abs(levels - a[p, g]) >= 10]
            a[p, g + 8] = far[np.random.randint(len(far))]
    return np.exp2(a.ravel()).repeat(32)


def f64(x):
    return np.asarray(x).astype(np.float64)


def striped(idx):
    return np.tile(np.asarray(idx).reshape(-1, 16).T, (8, 1)).astype(np.uint16)


def unstriped(offs):
    return offs[:16].T.reshape(-1).astype(np.int64)


E2M1 = np.array([0.0, 0.5, 1.0, 1.5, 2.0, 3.0, 4.0, 6.0, -0.0, -0.5, -1.0, -1.5, -2.0, -3.0, -4.0, -6.0])


def pack_weight(w, fmt):
    k, n = w.shape
    w = f64(np.asarray(w, np.float32).astype(ml_dtypes.bfloat16)).reshape(k // 32, 32, n)
    amax = np.abs(w).max(1)
    if fmt == "e4m3":
        byte = np.frexp(amax)[1] - 1 + 127 - 7
    else:
        mant, ex = np.frexp(amax / 6.0)
        byte = np.where(mant > 0.5, ex, ex - 1) + 127
    byte = np.clip(np.where(amax > 0, byte, 1), 1, 254)
    scaled = (w * np.exp2(127.0 - byte)[:, None, :]).reshape(k, n).astype(np.float32)
    by_word = np.ascontiguousarray(scaled.reshape(k // 512, 128, 4, n).transpose(0, 1, 3, 2))
    if fmt == "e4m3":
        words = by_word.astype(ml_dtypes.float8_e4m3fn).view(np.uint8)
    else:
        c = by_word.astype(ml_dtypes.float4_e2m1fn).view(np.uint8) & 0xF
        words = (c[..., 0::2] | (c[..., 1::2] << 4)).reshape(k // 512, 128, 2 * n)
    return np.ascontiguousarray(words), np.ascontiguousarray(byte.astype(np.uint8).reshape(k // 512, 16, n))


def unpack_weight(words, scales, fmt):
    g, _, n = scales.shape
    words = np.ascontiguousarray(words).reshape(g, 128, n, -1)
    if fmt == "e4m3":
        vals = words.view(ml_dtypes.float8_e4m3fn).astype(np.float64)
    else:
        nib = np.empty((g, 128, n, 4), np.uint8)
        nib[..., 0::2] = words & 0xF
        nib[..., 1::2] = words >> 4
        vals = E2M1[nib]
    vals = vals * np.repeat(np.exp2(scales.astype(np.float64) - 127.0), 8, axis=1)[..., None]
    return vals.transpose(0, 1, 3, 2).reshape(g * 512, n)


def bf(x):
    return np.asarray(x, np.float32).astype(ml_dtypes.bfloat16)


def planes(Y):
    r, m = Y.shape
    b = f64(bf(Y)).reshape(r // 32, 32, m)
    amax = np.abs(b).max(1)
    byte = np.clip(np.where(amax > 0, np.frexp(amax)[1] - 1 + 127 - 7, 1), 1, 254)
    codes = (b * np.exp2(127.0 - byte)[:, None, :]).reshape(r, m).astype(np.float32).astype(ml_dtypes.float8_e4m3fn).view(np.uint8)
    words = codes.reshape(r // 512, 128, 4, m).transpose(0, 1, 3, 2)
    return np.ascontiguousarray(words), np.ascontiguousarray(byte.astype(np.uint8).reshape(r // 512, 16, m))


D, T, I, J, U, M = 512, 2048, 512, 512, 1024, 1024


def setup_inputs():
    n = np.random.standard_normal
    idx = np.random.permutation(T)[:I]
    idx2 = np.random.permutation(U)[:J]
    idx3 = np.random.permutation(U)[:J]
    idx4 = np.random.permutation(M)[:J]
    fd = mx_kscale(D)
    keysp = pack_weight(n((D, T)) / fd[:, None], "e2m1")
    return {
        "keys_words": keysp[0],
        "keys_scales": keysp[1],
        "notes": (n((D, U)) * 1.0 / np.sqrt(D) * fd[:, None]).astype(np.float32),
        "old": (1.0 * n((I, M))).astype(np.float32),
        "fade": (np.random.uniform(0.3, 0.9, (I, 1))).astype(np.float32),
        "offs": striped(idx),
        "offs2": striped(idx2),
        "offs3": striped(idx3),
        "offs4": striped(idx4),
    }


def reference(keys_words, keys_scales, notes, old, fade, offs, offs2, offs3, offs4):
    idx = unstriped(offs)
    idx2 = unstriped(offs2)
    idx3 = unstriped(offs3)
    idx4 = unstriped(offs4)
    keysu = unpack_weight(keys_words, keys_scales, "e2m1")
    keysidxg = keysu[:, idx]
    notesq = mxq(f64(notes), 0, "e4m3")
    g1 = keysidxg.T @ notesq
    g9 = g1[:, idx2] - g1[:, idx3]
    g0 = np.tanh(g9)
    gf = np.zeros((I, M))
    gf[:, idx4] = g0
    y = f64(old) * f64(fade) + gf
    words, scales = planes(y)
    return y, words, scales

@@ -1,0 +1,199 @@
+from contextlib import ExitStack
+
+import concourse.mybir as mybir
+
+D, T, I, J, U, M = 512, 2048, 512, 512, 1024, 1024
+FLOPS = 2 * D * I * U
+
+F32 = mybir.dt.float32
+BF16 = mybir.dt.bfloat16
+I32 = mybir.dt.int32
+U32 = mybir.dt.uint32
+U16 = mybir.dt.uint16
+U8 = mybir.dt.uint8
+FP8X4 = mybir.dt.float8_e4m3fn_x4
+FP4X4 = mybir.dt.float4_e2m1fn_x4
+ALU = mybir.AluOpType
+ACT = mybir.ActivationFunctionType
+
+P = 128
+PACK = 4
+CHUNK = 256
+BANK = 512
+
+
+def interleave(copy, dst, src):
+    copy(dst.rearrange("p (c i) r -> p c r i", i=4), src.rearrange("p r (c i) -> p c r i", i=4))
+
+
+def tile_attend_tab_looked_keep_pl_kernel(
+    tc, keys_words, keys_scales, notes, old, fade, offs, offs2, offs3, offs4, out_0, out_1, out_2
+):
+    nc = tc.nc
+    with ExitStack() as ctx:
+        sb = ctx.enter_context(tc.tile_pool(name="sb", bufs=1))
+        psum = ctx.enter_context(tc.psum_pool(name="psum", bufs=1))
+
+        list1 = sb.tile([P, I // 16], U16, name="list1")
+        list2 = sb.tile([P, J // 16], U16, name="list2")
+        list3 = sb.tile([P, J // 16], U16, name="list3")
+        list4 = sb.tile([P, J // 16], U16, name="list4")
+        pool_words = sb.tile([P, T], U16, name="pool_words", align_bytes=64)
+        pool_scales = sb.tile([P, T], U8, name="pool_scales", align_bytes=64)
+        n_chunks = U // CHUNK
+        raw = [sb.tile([P, PACK, CHUNK], F32, name="raw%d" % c) for c in range(n_chunks)]
+        old_sb = [sb.tile([P, M], F32, name="old%d" % r) for r in range(PACK)]
+        fade_sb = sb.tile([P, PACK], F32, name="fade_sb")
+        placed = {r: sb.tile([P, M], F32, name="placed%d" % r) for r in (0, 1, 3)}
+
+        notes_v = notes.rearrange("(p r) u -> p r u", r=PACK)
+        old_v = old.rearrange("(p r) m -> p r m", r=PACK)
+        out_v = out_0.rearrange("(p r) m -> p r m", r=PACK)
+
+        nc.vector.memset(pool_scales[:].bitcast(I32), 0)
+        nc.sync.dma_start(list1[:], offs)
+        nc.sync.dma_start(list3[:], offs3)
+        nc.sync.dma_start(list2[:], offs2)
+        nc.sync.dma_start(list4[:], offs4)
+        nc.sync.dma_start(fade_sb[:], fade.rearrange("(p r) o -> p (r o)", r=PACK))
+        nc.sync.dma_start(pool_words[:].bitcast(I32), keys_words[0].bitcast(I32))
+        nc.sync.dma_start(raw[0][:], notes_v[:, :, :CHUNK])
+        for q in range(4):
+            nc.sync.dma_start(
+                pool_scales[32 * q : 32 * q + 4, :].bitcast(I32), keys_scales[0, 4 * q : 4 * q + 4, :].bitcast(I32)
+            )
+        for c in range(1, n_chunks):
+            nc.sync.dma_start(raw[c][:], notes_v[:, :, c * CHUNK : (c + 1) * CHUNK])
+        for r in range(PACK):
+            nc.sync.dma_start(old_sb[r][:], old_v[:, r, :])
+        for r in (0, 1, 3):
+            nc.vector.memset(placed[r][:], 0.0)
+
+        picked_words = sb.tile([P, I], U16, name="picked_words", align_bytes=64)
+        picked_scales = sb.tile([P, I], U8, name="picked_scales", align_bytes=64)
+        key_words = sb.tile([P, I], U16, name="key_words", align_bytes=64)
+        key_scales = sb.tile([P, I], U8, name="key_scales", align_bytes=64)
+        nc.vector.tensor_copy(picked_words[:], pool_words[:].indirect(list1[:]))
+        nc.vector.tensor_copy(picked_scales[:], pool_scales[:].indirect(list1[:]))
+        nc.vector.tensor_copy(
+            key_words[:].rearrange("p (r s) -> p r s", r=PACK), picked_words[:].rearrange("p (s r) -> p r s", r=PACK)
+        )
+        nc.vector.tensor_copy(
+            key_scales[:].rearrange("p (r s) -> p r s", r=PACK), picked_scales[:].rearrange("p (s r) -> p r s", r=PACK)
+        )
+
+        grouped = [sb.tile([P, CHUNK, PACK], BF16, name="grouped%d" % c, align_bytes=64) for c in range(n_chunks)]
+        note_codes = [sb.tile([P, CHUNK], U32, name="note_codes%d" % c, align_bytes=64) for c in range(n_chunks)]
+        note_scales = [sb.tile([P, CHUNK], U8, name="note_scales%d" % c, align_bytes=64) for c in range(n_chunks)]
+        banks = [[psum.tile([P, BANK], F32, name="bank%d_%d" % (r, h)) for h in range(2)] for r in range(PACK)]
+        wide = [sb.tile([P, U], F32, name="wide%d" % r) for r in range(PACK)]
+
+        def quantise(c):
+            nc.vector.quantize_mx(
+                out=note_codes[c][:].bitcast(FP8X4),
+                scales=note_scales[c][:],
+                in_=grouped[c][:].rearrange("p c r -> p (c r)"),
+            )
+
+        for c in range(3):
+            interleave(nc.scalar.copy, grouped[c][:], raw[c][:])
+        quantise(0)
+        quantise(1)
+        interleave(nc.vector.tensor_copy, grouped[3][:], raw[3][:])
+        quantise(2)
+        quantise(3)
+        for r in range(PACK):
+            for c in range(n_chunks):
+                nc.tensor.matmul_mx(
+                    out=banks[r][c // 2][:, (c % 2) * CHUNK : (c % 2 + 1) * CHUNK],
+                    lhsT=key_words[:, r * P : (r + 1) * P].bitcast(FP4X4),
+                    lhsT_scale=key_scales[:, r * P : (r + 1) * P],
+                    rhs=note_codes[c][:].bitcast(FP8X4),
+                    rhs_scale=note_scales[c][:],
+                    start=True,
+                    stop=True,
+                )
+        for r in range(PACK):
+            nc.scalar.copy(wide[r][:, :BANK], banks[r][0][:])
+        for r in range(PACK):
+            nc.vector.tensor_copy(wide[r][:, BANK:], banks[r][1][:])
+
+        minus = [sb.tile([P, J], F32, name="minus%d" % r) for r in range(PACK)]
+        diff = [sb.tile([P, J], F32, name="diff%d" % r) for r in range(PACK)]
+        table = [sb.tile([P, J], F32, name="table%d" % r) for r in range(PACK)]
+        y = [sb.tile([P, PACK, BANK], F32, name="y%d" % h) for h in range(2)]
+
+        def look_up_minus(r):
+            nc.scalar.activation(minus[r][:], wide[r][:].indirect(list3[:]), ACT.Copy)
+
+        def look_up_diff(r):
+            nc.vector.tensor_tensor(diff[r][:], wide[r][:].indirect(list2[:]), minus[r][:], ALU.subtract)
+
+        def squash(r):
+            nc.scalar.activation(table[r][:], diff[r][:], ACT.Tanh)
+
+        def place_vector(r):
+            nc.vector.tensor_copy(placed[r][:].indirect(list4[:]), table[r][:])
+
+        def place_scalar(r):
+            for h in range(2):
+                nc.scalar.activation(
+                    placed[r][:].indirect(list4[:, 16 * h : 16 * h + 16]), table[r][:, 256 * h : 256 * h + 256], ACT.Copy
+                )
+
+        def combine(r, first, width):
+            cols = slice(first, first + width)
+            nc.vector.scalar_tensor_tensor(
+                y[first // BANK][:, r, first % BANK : first % BANK + width],
+                old_sb[r][:, cols],
+                fade_sb[:, r : r + 1],
+                placed[r][:, cols],
+                ALU.mult,
+                ALU.add,
+            )
+
+        for r in range(PACK):
+            look_up_minus(r)
+        for r in range(PACK):
+            look_up_diff(r)
+        squash(0)
+        squash(1)
+        place_vector(0)
+        place_scalar(1)
+        squash(2)
+        squash(3)
+        for r in range(2):
+            for h in range(2):
+                combine(r, h * BANK, BANK)
+                nc.sync.dma_start(out_v[:, r, h * BANK : (h + 1) * BANK], y[h][:, r, :])
+        placed[2] = sb.tile([P, M], F32, name="placed0")
+        nc.gpsimd.memset(placed[2][:], 0.0)
+        place_vector(2)
+        place_scalar(3)
+
+        y_codes = sb.tile([P, M], U32, name="y_codes", align_bytes=64)
+        y_scales = sb.tile([P, M], U8, name="y_scales", align_bytes=64)
+        y_grouped = [sb.tile([P, CHUNK, PACK], BF16, name="y_grouped%d" % c, align_bytes=64) for c in range(4)]
+        words_v = out_1[0].rearrange("p c r -> p (c r)").bitcast(I32)
+        combine(2, 0, BANK)
+        combine(3, 0, CHUNK)
+        combine(3, CHUNK, CHUNK)
+        nc.sync.dma_start(out_v[:, 2:, :BANK], y[0][:, 2:, :])
+        combine(2, BANK, BANK)
+        combine(3, BANK, BANK)
+        nc.sync.dma_start(out_v[:, 2:, BANK:], y[1][:, 2:, :])
+        for c in (0, 1, 3, 2):
+            cols = slice((c % 2) * CHUNK, (c % 2 + 1) * CHUNK)
+            interleave(nc.scalar.copy if c < 3 else nc.vector.tensor_copy, y_grouped[c][:], y[c // 2][:, :, cols])
+        for c in (0, 1, 3, 2):
+            cols = slice(c * CHUNK, (c + 1) * CHUNK)
+            nc.vector.quantize_mx(
+                out=y_codes[:, cols].bitcast(FP8X4),
+                scales=y_scales[:, cols],
+                in_=y_grouped[c][:].rearrange("p c r -> p (c r)"),
+            )
+            nc.sync.dma_start(words_v[:, cols], y_codes[:, cols].bitcast(I32))
+        for q in range(4):
+            (nc.scalar if q % 2 else nc.sync).dma_start(
+                out_2[0, 4 * q : 4 * q + 4, :].bitcast(I32), y_scales[32 * q : 32 * q + 4, :].bitcast(I32)
+            )

@@ -44,7 +44,7 @@ def tile_attend_tab_looked_keep_pl_kernel(
         raw = [sb.tile([P, PACK, CHUNK], F32, name="raw%d" % c) for c in range(n_chunks)]
         old_sb = [sb.tile([P, M], F32, name="old%d" % r) for r in range(PACK)]
         fade_sb = sb.tile([P, PACK], F32, name="fade_sb")
-        placed = {r: sb.tile([P, M], F32, name="placed%d" % r) for r in (0, 1, 3)}
+        placed = [sb.tile([P, M], F32, name="placed%d" % r) for r in range(PACK)]
 
         notes_v = notes.rearrange("(p r) u -> p r u", r=PACK)
         old_v = old.rearrange("(p r) m -> p r m", r=PACK)
@@ -55,19 +55,17 @@ def tile_attend_tab_looked_keep_pl_kernel(
         nc.sync.dma_start(list3[:], offs3)
         nc.sync.dma_start(list2[:], offs2)
         nc.sync.dma_start(list4[:], offs4)
-        nc.sync.dma_start(fade_sb[:], fade.rearrange("(p r) o -> p (r o)", r=PACK))
         nc.sync.dma_start(pool_words[:].bitcast(I32), keys_words[0].bitcast(I32))
         nc.sync.dma_start(raw[0][:], notes_v[:, :, :CHUNK])
-        for q in range(4):
-            nc.sync.dma_start(
-                pool_scales[32 * q : 32 * q + 4, :].bitcast(I32), keys_scales[0, 4 * q : 4 * q + 4, :].bitcast(I32)
-            )
+        for k in range(4):
+            nc.sync.dma_start(pool_scales[k:P:32, :].bitcast(I32), keys_scales[0, k:16:4, :].bitcast(I32))
         for c in range(1, n_chunks):
             nc.sync.dma_start(raw[c][:], notes_v[:, :, c * CHUNK : (c + 1) * CHUNK])
+        nc.sync.dma_start(fade_sb[:], fade.rearrange("(p r) o -> p (r o)", r=PACK))
         for r in range(PACK):
             nc.sync.dma_start(old_sb[r][:], old_v[:, r, :])
-        for r in (0, 1, 3):
-            nc.vector.memset(placed[r][:], 0.0)
+        for r in range(PACK):
+            (nc.vector if r < 2 else nc.gpsimd).memset(placed[r][:], 0.0)
 
         picked_words = sb.tile([P, I], U16, name="picked_words", align_bytes=64)
         picked_scales = sb.tile([P, I], U8, name="picked_scales", align_bytes=64)
@@ -113,7 +111,7 @@ def tile_attend_tab_looked_keep_pl_kernel(
                     start=True,
                     stop=True,
                 )
-        for r in range(PACK):
+        for r in range(3):
             nc.scalar.copy(wide[r][:, :BANK], banks[r][0][:])
         for r in range(PACK):
             nc.vector.tensor_copy(wide[r][:, BANK:], banks[r][1][:])
@@ -132,14 +130,12 @@ def tile_attend_tab_looked_keep_pl_kernel(
         def squash(r):
             nc.scalar.activation(table[r][:], diff[r][:], ACT.Tanh)
 
-        def place_vector(r):
-            nc.vector.tensor_copy(placed[r][:].indirect(list4[:]), table[r][:])
-
-        def place_scalar(r):
-            for h in range(2):
-                nc.scalar.activation(
-                    placed[r][:].indirect(list4[:, 16 * h : 16 * h + 16]), table[r][:, 256 * h : 256 * h + 256], ACT.Copy
-                )
+        def place(engine, r, first, count):
+            window = placed[r][:].indirect(list4[:, first // 16 : (first + count) // 16])
+            if engine is nc.vector:
+                nc.vector.tensor_copy(window, table[r][:, first : first + count])
+            else:
+                nc.scalar.activation(window, table[r][:, first : first + count], ACT.Copy)
 
         def combine(r, first, width):
             cols = slice(first, first + width)
@@ -152,40 +148,41 @@ def tile_attend_tab_looked_keep_pl_kernel(
                 ALU.add,
             )
 
-        for r in range(PACK):
+        look_up_minus(0)
+        nc.scalar.copy(wide[3][:, :BANK], banks[3][0][:])
+        for r in range(1, PACK):
             look_up_minus(r)
         for r in range(PACK):
             look_up_diff(r)
+        half = J // 2
         squash(0)
         squash(1)
-        place_vector(0)
-        place_scalar(1)
+        place(nc.vector, 0, 0, J)
+        place(nc.scalar, 1, 0, half)
         squash(2)
+        place(nc.scalar, 1, half, half)
         squash(3)
-        for r in range(2):
+        place(nc.vector, 3, 0, half)
+        place(nc.scalar, 2, 0, half)
+        place(nc.scalar, 2, half, half)
+        place(nc.scalar, 3, half, half)
+        for r in range(3):
             for h in range(2):
                 combine(r, h * BANK, BANK)
                 nc.sync.dma_start(out_v[:, r, h * BANK : (h + 1) * BANK], y[h][:, r, :])
-        placed[2] = sb.tile([P, M], F32, name="placed0")
-        nc.gpsimd.memset(placed[2][:], 0.0)
-        place_vector(2)
-        place_scalar(3)
 
         y_codes = sb.tile([P, M], U32, name="y_codes", align_bytes=64)
         y_scales = sb.tile([P, M], U8, name="y_scales", align_bytes=64)
         y_grouped = [sb.tile([P, CHUNK, PACK], BF16, name="y_grouped%d" % c, align_bytes=64) for c in range(4)]
         words_v = out_1[0].rearrange("p c r -> p (c r)").bitcast(I32)
-        combine(2, 0, BANK)
-        combine(3, 0, CHUNK)
-        combine(3, CHUNK, CHUNK)
-        nc.sync.dma_start(out_v[:, 2:, :BANK], y[0][:, 2:, :])
-        combine(2, BANK, BANK)
-        combine(3, BANK, BANK)
-        nc.sync.dma_start(out_v[:, 2:, BANK:], y[1][:, 2:, :])
-        for c in (0, 1, 3, 2):
+        for h in range(2):
+            combine(3, h * BANK, CHUNK)
+            combine(3, h * BANK + CHUNK, CHUNK)
+            nc.sync.dma_start(out_v[:, 3, h * BANK : (h + 1) * BANK], y[h][:, 3, :])
+        for c in range(4):
             cols = slice((c % 2) * CHUNK, (c % 2 + 1) * CHUNK)
-            interleave(nc.scalar.copy if c < 3 else nc.vector.tensor_copy, y_grouped[c][:], y[c // 2][:, :, cols])
-        for c in (0, 1, 3, 2):
+            interleave(nc.scalar.copy if c < 2 else nc.vector.tensor_copy, y_grouped[c][:], y[c // 2][:, :, cols])
+        for c in (0, 2, 3, 1):
             cols = slice(c * CHUNK, (c + 1) * CHUNK)
             nc.vector.quantize_mx(
                 out=y_codes[:, cols].bitcast(FP8X4),
@@ -193,7 +190,7 @@ def tile_attend_tab_looked_keep_pl_kernel(
                 in_=y_grouped[c][:].rearrange("p c r -> p (c r)"),
             )
             nc.sync.dma_start(words_v[:, cols], y_codes[:, cols].bitcast(I32))
-        for q in range(4):
-            (nc.scalar if q % 2 else nc.sync).dma_start(
-                out_2[0, 4 * q : 4 * q + 4, :].bitcast(I32), y_scales[32 * q : 32 * q + 4, :].bitcast(I32)
+        for k in range(4):
+            (nc.scalar if k % 2 else nc.sync).dma_start(
+                out_2[0, k:16:4, :].bitcast(I32), y_scales[k:P:32, :].bitcast(I32)
             )

@@ -18,12 +18,28 @@ ACT = mybir.ActivationFunctionType
 
 P = 128
 PACK = 4
-CHUNK = 256
+QUADRANT = 32
+SCALE_ROWS = 4
+BLOCKS = 16
+PER_COLUMN = 16
 BANK = 512
+CHUNK = 256
+CHUNKS = U // CHUNK
+LAST = PACK - 1
+HALF_LIST = J // 2
+VECTOR_SHARE = 384
 
 
 def interleave(copy, dst, src):
-    copy(dst.rearrange("p (c i) r -> p c r i", i=4), src.rearrange("p r (c i) -> p c r i", i=4))
+    copy(dst.rearrange("p (c n) r -> p c r n", n=4), src.rearrange("p r (c n) -> p c r n", n=4))
+
+
+def chunk_columns(c):
+    return slice(c * CHUNK, (c + 1) * CHUNK)
+
+
+def half_columns(h):
+    return slice(h * BANK, (h + 1) * BANK)
 
 
 def tile_attend_tab_looked_keep_pl_kernel(
@@ -34,14 +50,13 @@ def tile_attend_tab_looked_keep_pl_kernel(
         sb = ctx.enter_context(tc.tile_pool(name="sb", bufs=1))
         psum = ctx.enter_context(tc.psum_pool(name="psum", bufs=1))
 
-        list1 = sb.tile([P, I // 16], U16, name="list1")
-        list2 = sb.tile([P, J // 16], U16, name="list2")
-        list3 = sb.tile([P, J // 16], U16, name="list3")
-        list4 = sb.tile([P, J // 16], U16, name="list4")
+        list1 = sb.tile([P, I // PER_COLUMN], U16, name="list1")
+        list2 = sb.tile([P, J // PER_COLUMN], U16, name="list2")
+        list3 = sb.tile([P, J // PER_COLUMN], U16, name="list3")
+        list4 = sb.tile([P, J // PER_COLUMN], U16, name="list4")
         pool_words = sb.tile([P, T], U16, name="pool_words", align_bytes=64)
         pool_scales = sb.tile([P, T], U8, name="pool_scales", align_bytes=64)
-        n_chunks = U // CHUNK
-        raw = [sb.tile([P, PACK, CHUNK], F32, name="raw%d" % c) for c in range(n_chunks)]
+        raw = [sb.tile([P, PACK, CHUNK], F32, name="raw%d" % c) for c in range(CHUNKS)]
         old_sb = [sb.tile([P, M], F32, name="old%d" % r) for r in range(PACK)]
         fade_sb = sb.tile([P, PACK], F32, name="fade_sb")
         placed = [sb.tile([P, M], F32, name="placed%d" % r) for r in range(PACK)]
@@ -50,22 +65,24 @@ def tile_attend_tab_looked_keep_pl_kernel(
         old_v = old.rearrange("(p r) m -> p r m", r=PACK)
         out_v = out_0.rearrange("(p r) m -> p r m", r=PACK)
 
-        nc.vector.memset(pool_scales[:].bitcast(I32), 0)
+        nc.gpsimd.memset(pool_scales[:].bitcast(I32), 0)
         nc.sync.dma_start(list1[:], offs)
         nc.sync.dma_start(list3[:], offs3)
         nc.sync.dma_start(list2[:], offs2)
         nc.sync.dma_start(list4[:], offs4)
         nc.sync.dma_start(pool_words[:].bitcast(I32), keys_words[0].bitcast(I32))
-        nc.sync.dma_start(raw[0][:], notes_v[:, :, :CHUNK])
-        for k in range(4):
-            nc.sync.dma_start(pool_scales[k:P:32, :].bitcast(I32), keys_scales[0, k:16:4, :].bitcast(I32))
-        for c in range(1, n_chunks):
-            nc.sync.dma_start(raw[c][:], notes_v[:, :, c * CHUNK : (c + 1) * CHUNK])
+        nc.sync.dma_start(raw[0][:], notes_v[:, :, chunk_columns(0)])
+        for k in range(SCALE_ROWS):
+            nc.sync.dma_start(
+                pool_scales[k:P:QUADRANT, :].bitcast(I32), keys_scales[0, k:BLOCKS:SCALE_ROWS, :].bitcast(I32)
+            )
+        for c in range(1, CHUNKS):
+            nc.sync.dma_start(raw[c][:], notes_v[:, :, chunk_columns(c)])
         nc.sync.dma_start(fade_sb[:], fade.rearrange("(p r) o -> p (r o)", r=PACK))
         for r in range(PACK):
             nc.sync.dma_start(old_sb[r][:], old_v[:, r, :])
         for r in range(PACK):
-            (nc.vector if r < 2 else nc.gpsimd).memset(placed[r][:], 0.0)
+            (nc.vector if r < PACK // 2 else nc.gpsimd).memset(placed[r][:], 0.0)
 
         picked_words = sb.tile([P, I], U16, name="picked_words", align_bytes=64)
         picked_scales = sb.tile([P, I], U8, name="picked_scales", align_bytes=64)
@@ -73,37 +90,35 @@ def tile_attend_tab_looked_keep_pl_kernel(
         key_scales = sb.tile([P, I], U8, name="key_scales", align_bytes=64)
         nc.vector.tensor_copy(picked_words[:], pool_words[:].indirect(list1[:]))
         nc.vector.tensor_copy(picked_scales[:], pool_scales[:].indirect(list1[:]))
-        nc.vector.tensor_copy(
-            key_words[:].rearrange("p (r s) -> p r s", r=PACK), picked_words[:].rearrange("p (s r) -> p r s", r=PACK)
-        )
-        nc.vector.tensor_copy(
-            key_scales[:].rearrange("p (r s) -> p r s", r=PACK), picked_scales[:].rearrange("p (s r) -> p r s", r=PACK)
-        )
+        for dealt, picked in ((key_words, picked_words), (key_scales, picked_scales)):
+            nc.vector.tensor_copy(
+                dealt[:].rearrange("p (r s) -> p r s", r=PACK), picked[:].rearrange("p (s r) -> p r s", r=PACK)
+            )
 
-        grouped = [sb.tile([P, CHUNK, PACK], BF16, name="grouped%d" % c, align_bytes=64) for c in range(n_chunks)]
-        note_codes = [sb.tile([P, CHUNK], U32, name="note_codes%d" % c, align_bytes=64) for c in range(n_chunks)]
-        note_scales = [sb.tile([P, CHUNK], U8, name="note_scales%d" % c, align_bytes=64) for c in range(n_chunks)]
+        grouped = [sb.tile([P, CHUNK, PACK], BF16, name="grouped%d" % c, align_bytes=64) for c in range(CHUNKS)]
+        note_codes = [sb.tile([P, CHUNK], U32, name="note_codes%d" % c, align_bytes=64) for c in range(CHUNKS)]
+        note_scales = [sb.tile([P, CHUNK], U8, name="note_scales%d" % c, align_bytes=64) for c in range(CHUNKS)]
         banks = [[psum.tile([P, BANK], F32, name="bank%d_%d" % (r, h)) for h in range(2)] for r in range(PACK)]
         wide = [sb.tile([P, U], F32, name="wide%d" % r) for r in range(PACK)]
 
-        def quantise(c):
+        def quantise_notes(c):
             nc.vector.quantize_mx(
                 out=note_codes[c][:].bitcast(FP8X4),
                 scales=note_scales[c][:],
                 in_=grouped[c][:].rearrange("p c r -> p (c r)"),
             )
 
-        for c in range(3):
+        for c in range(CHUNKS - 1):
             interleave(nc.scalar.copy, grouped[c][:], raw[c][:])
-        quantise(0)
-        quantise(1)
-        interleave(nc.vector.tensor_copy, grouped[3][:], raw[3][:])
-        quantise(2)
-        quantise(3)
+        quantise_notes(0)
+        quantise_notes(1)
+        interleave(nc.vector.tensor_copy, grouped[CHUNKS - 1][:], raw[CHUNKS - 1][:])
+        quantise_notes(2)
+        quantise_notes(3)
         for r in range(PACK):
-            for c in range(n_chunks):
+            for c in range(CHUNKS):
                 nc.tensor.matmul_mx(
-                    out=banks[r][c // 2][:, (c % 2) * CHUNK : (c % 2 + 1) * CHUNK],
+                    out=banks[r][c // 2][:, chunk_columns(c % 2)],
                     lhsT=key_words[:, r * P : (r + 1) * P].bitcast(FP4X4),
                     lhsT_scale=key_scales[:, r * P : (r + 1) * P],
                     rhs=note_codes[c][:].bitcast(FP8X4),
@@ -111,10 +126,10 @@ def tile_attend_tab_looked_keep_pl_kernel(
                     start=True,
                     stop=True,
                 )
-        for r in range(3):
-            nc.scalar.copy(wide[r][:, :BANK], banks[r][0][:])
+        for r in range(LAST):
+            nc.scalar.copy(wide[r][:, half_columns(0)], banks[r][0][:])
         for r in range(PACK):
-            nc.vector.tensor_copy(wide[r][:, BANK:], banks[r][1][:])
+            nc.vector.tensor_copy(wide[r][:, half_columns(1)], banks[r][1][:])
 
         minus = [sb.tile([P, J], F32, name="minus%d" % r) for r in range(PACK)]
         diff = [sb.tile([P, J], F32, name="diff%d" % r) for r in range(PACK)]
@@ -130,12 +145,14 @@ def tile_attend_tab_looked_keep_pl_kernel(
         def squash(r):
             nc.scalar.activation(table[r][:], diff[r][:], ACT.Tanh)
 
-        def place(engine, r, first, count):
-            window = placed[r][:].indirect(list4[:, first // 16 : (first + count) // 16])
-            if engine is nc.vector:
-                nc.vector.tensor_copy(window, table[r][:, first : first + count])
-            else:
-                nc.scalar.activation(window, table[r][:, first : first + count], ACT.Copy)
+        def places(r, first, count):
+            return placed[r][:].indirect(list4[:, first // PER_COLUMN : (first + count) // PER_COLUMN])
+
+        def place_by_vector(r, first, count):
+            nc.vector.tensor_copy(places(r, first, count), table[r][:, first : first + count])
+
+        def place_by_scalar(r, first, count):
+            nc.scalar.activation(places(r, first, count), table[r][:, first : first + count], ACT.Copy)
 
         def combine(r, first, width):
             cols = slice(first, first + width)
@@ -148,49 +165,59 @@ def tile_attend_tab_looked_keep_pl_kernel(
                 ALU.add,
             )
 
+        def store(r, h):
+            nc.sync.dma_start(out_v[:, r, half_columns(h)], y[h][:, r, :])
+
         look_up_minus(0)
-        nc.scalar.copy(wide[3][:, :BANK], banks[3][0][:])
+        nc.scalar.copy(wide[LAST][:, half_columns(0)], banks[LAST][0][:])
         for r in range(1, PACK):
             look_up_minus(r)
         for r in range(PACK):
             look_up_diff(r)
-        half = J // 2
+
         squash(0)
         squash(1)
-        place(nc.vector, 0, 0, J)
-        place(nc.scalar, 1, 0, half)
+        place_by_vector(0, 0, J)
+        place_by_scalar(1, 0, HALF_LIST)
         squash(2)
-        place(nc.scalar, 1, half, half)
-        squash(3)
-        place(nc.vector, 3, 0, half)
-        place(nc.scalar, 2, 0, half)
-        place(nc.scalar, 2, half, half)
-        place(nc.scalar, 3, half, half)
-        for r in range(3):
+        squash(LAST)
+        place_by_vector(LAST, 0, VECTOR_SHARE)
+        place_by_scalar(2, 0, HALF_LIST)
+        place_by_scalar(1, HALF_LIST, HALF_LIST)
+        place_by_scalar(2, HALF_LIST, HALF_LIST)
+        place_by_scalar(LAST, VECTOR_SHARE, J - VECTOR_SHARE)
+
+        faded = sb.tile([P, M], F32, name="wide%d" % LAST)
+        nc.gpsimd.tensor_scalar(faded[:], old_sb[0][:], fade_sb[:, 0:1], 0.0, ALU.mult, ALU.add)
+        for h in range(2):
+            cols = half_columns(h)
+            nc.gpsimd.tensor_tensor(y[h][:, 0, :], faded[:, cols], placed[0][:, cols], ALU.add)
+            store(0, h)
+        for r in range(1, LAST):
             for h in range(2):
                 combine(r, h * BANK, BANK)
-                nc.sync.dma_start(out_v[:, r, h * BANK : (h + 1) * BANK], y[h][:, r, :])
+                store(r, h)
 
         y_codes = sb.tile([P, M], U32, name="y_codes", align_bytes=64)
         y_scales = sb.tile([P, M], U8, name="y_scales", align_bytes=64)
-        y_grouped = [sb.tile([P, CHUNK, PACK], BF16, name="y_grouped%d" % c, align_bytes=64) for c in range(4)]
+        y_grouped = [sb.tile([P, CHUNK, PACK], BF16, name="y_grouped%d" % c, align_bytes=64) for c in range(CHUNKS)]
         words_v = out_1[0].rearrange("p c r -> p (c r)").bitcast(I32)
         for h in range(2):
-            combine(3, h * BANK, CHUNK)
-            combine(3, h * BANK + CHUNK, CHUNK)
-            nc.sync.dma_start(out_v[:, 3, h * BANK : (h + 1) * BANK], y[h][:, 3, :])
-        for c in range(4):
-            cols = slice((c % 2) * CHUNK, (c % 2 + 1) * CHUNK)
-            interleave(nc.scalar.copy if c < 2 else nc.vector.tensor_copy, y_grouped[c][:], y[c // 2][:, :, cols])
+            combine(LAST, h * BANK, CHUNK)
+            combine(LAST, h * BANK + CHUNK, CHUNK)
+            store(LAST, h)
+        for c in range(CHUNKS):
+            copy = nc.scalar.copy if c < CHUNKS // 2 else nc.vector.tensor_copy
+            interleave(copy, y_grouped[c][:], y[c // 2][:, :, chunk_columns(c % 2)])
         for c in (0, 2, 3, 1):
-            cols = slice(c * CHUNK, (c + 1) * CHUNK)
+            cols = chunk_columns(c)
             nc.vector.quantize_mx(
                 out=y_codes[:, cols].bitcast(FP8X4),
                 scales=y_scales[:, cols],
                 in_=y_grouped[c][:].rearrange("p c r -> p (c r)"),
             )
             nc.sync.dma_start(words_v[:, cols], y_codes[:, cols].bitcast(I32))
-        for k in range(4):
+        for k in range(SCALE_ROWS):
             (nc.scalar if k % 2 else nc.sync).dma_start(
-                out_2[0, k:16:4, :].bitcast(I32), y_scales[k:P:32, :].bitcast(I32)
+                out_2[0, k:BLOCKS:SCALE_ROWS, :].bitcast(I32), y_scales[k:P:QUADRANT, :].bitcast(I32)
             )

from contextlib import ExitStack

import concourse.mybir as mybir

D, T, I, J, U, M = 512, 2048, 512, 512, 1024, 1024
FLOPS = 2 * D * I * U

F32 = mybir.dt.float32
BF16 = mybir.dt.bfloat16
I32 = mybir.dt.int32
U32 = mybir.dt.uint32
U16 = mybir.dt.uint16
U8 = mybir.dt.uint8
FP8X4 = mybir.dt.float8_e4m3fn_x4
FP4X4 = mybir.dt.float4_e2m1fn_x4
ALU = mybir.AluOpType
ACT = mybir.ActivationFunctionType

P = 128
PACK = 4
QUADRANT = 32
SCALE_ROWS = 4
BLOCKS = 16
PER_COLUMN = 16
BANK = 512
CHUNK = 256
CHUNKS = U // CHUNK
LAST = PACK - 1
HALF_LIST = J // 2
VECTOR_SHARE = 384


def interleave(copy, dst, src):
    copy(dst.rearrange("p (c n) r -> p c r n", n=4), src.rearrange("p r (c n) -> p c r n", n=4))


def chunk_columns(c):
    return slice(c * CHUNK, (c + 1) * CHUNK)


def half_columns(h):
    return slice(h * BANK, (h + 1) * BANK)


def tile_attend_tab_looked_keep_pl_kernel(
    tc, keys_words, keys_scales, notes, old, fade, offs, offs2, offs3, offs4, out_0, out_1, out_2
):
    nc = tc.nc
    with ExitStack() as ctx:
        sb = ctx.enter_context(tc.tile_pool(name="sb", bufs=1))
        psum = ctx.enter_context(tc.psum_pool(name="psum", bufs=1))

        list1 = sb.tile([P, I // PER_COLUMN], U16, name="list1")
        list2 = sb.tile([P, J // PER_COLUMN], U16, name="list2")
        list3 = sb.tile([P, J // PER_COLUMN], U16, name="list3")
        list4 = sb.tile([P, J // PER_COLUMN], U16, name="list4")
        pool_words = sb.tile([P, T], U16, name="pool_words", align_bytes=64)
        pool_scales = sb.tile([P, T], U8, name="pool_scales", align_bytes=64)
        raw = [sb.tile([P, PACK, CHUNK], F32, name="raw%d" % c) for c in range(CHUNKS)]
        old_sb = [sb.tile([P, M], F32, name="old%d" % r) for r in range(PACK)]
        fade_sb = sb.tile([P, PACK], F32, name="fade_sb")
        placed = [sb.tile([P, M], F32, name="placed%d" % r) for r in range(PACK)]

        notes_v = notes.rearrange("(p r) u -> p r u", r=PACK)
        old_v = old.rearrange("(p r) m -> p r m", r=PACK)
        out_v = out_0.rearrange("(p r) m -> p r m", r=PACK)

        nc.gpsimd.memset(pool_scales[:].bitcast(I32), 0)
        nc.sync.dma_start(list1[:], offs)
        nc.sync.dma_start(list3[:], offs3)
        nc.sync.dma_start(list2[:], offs2)
        nc.sync.dma_start(list4[:], offs4)
        nc.sync.dma_start(pool_words[:].bitcast(I32), keys_words[0].bitcast(I32))
        nc.sync.dma_start(raw[0][:], notes_v[:, :, chunk_columns(0)])
        for k in range(SCALE_ROWS):
            nc.sync.dma_start(
                pool_scales[k:P:QUADRANT, :].bitcast(I32), keys_scales[0, k:BLOCKS:SCALE_ROWS, :].bitcast(I32)
            )
        for c in range(1, CHUNKS):
            nc.sync.dma_start(raw[c][:], notes_v[:, :, chunk_columns(c)])
        nc.sync.dma_start(fade_sb[:], fade.rearrange("(p r) o -> p (r o)", r=PACK))
        for r in range(PACK):
            nc.sync.dma_start(old_sb[r][:], old_v[:, r, :])
        for r in range(PACK):
            (nc.vector if r < PACK // 2 else nc.gpsimd).memset(placed[r][:], 0.0)

        picked_words = sb.tile([P, I], U16, name="picked_words", align_bytes=64)
        picked_scales = sb.tile([P, I], U8, name="picked_scales", align_bytes=64)
        key_words = sb.tile([P, I], U16, name="key_words", align_bytes=64)
        key_scales = sb.tile([P, I], U8, name="key_scales", align_bytes=64)
        nc.vector.tensor_copy(picked_words[:], pool_words[:].indirect(list1[:]))
        nc.vector.tensor_copy(picked_scales[:], pool_scales[:].indirect(list1[:]))
        for dealt, picked in ((key_words, picked_words), (key_scales, picked_scales)):
            nc.vector.tensor_copy(
                dealt[:].rearrange("p (r s) -> p r s", r=PACK), picked[:].rearrange("p (s r) -> p r s", r=PACK)
            )

        grouped = [sb.tile([P, CHUNK, PACK], BF16, name="grouped%d" % c, align_bytes=64) for c in range(CHUNKS)]
        note_codes = [sb.tile([P, CHUNK], U32, name="note_codes%d" % c, align_bytes=64) for c in range(CHUNKS)]
        note_scales = [sb.tile([P, CHUNK], U8, name="note_scales%d" % c, align_bytes=64) for c in range(CHUNKS)]
        banks = [[psum.tile([P, BANK], F32, name="bank%d_%d" % (r, h)) for h in range(2)] for r in range(PACK)]
        wide = [sb.tile([P, U], F32, name="wide%d" % r) for r in range(PACK)]

        def quantise_notes(c):
            nc.vector.quantize_mx(
                out=note_codes[c][:].bitcast(FP8X4),
                scales=note_scales[c][:],
                in_=grouped[c][:].rearrange("p c r -> p (c r)"),
            )

        for c in range(CHUNKS - 1):
            interleave(nc.scalar.copy, grouped[c][:], raw[c][:])
        quantise_notes(0)
        quantise_notes(1)
        interleave(nc.vector.tensor_copy, grouped[CHUNKS - 1][:], raw[CHUNKS - 1][:])
        quantise_notes(2)
        quantise_notes(3)
        for r in range(PACK):
            for c in range(CHUNKS):
                nc.tensor.matmul_mx(
                    out=banks[r][c // 2][:, chunk_columns(c % 2)],
                    lhsT=key_words[:, r * P : (r + 1) * P].bitcast(FP4X4),
                    lhsT_scale=key_scales[:, r * P : (r + 1) * P],
                    rhs=note_codes[c][:].bitcast(FP8X4),
                    rhs_scale=note_scales[c][:],
                    start=True,
                    stop=True,
                )
        for r in range(LAST):
            nc.scalar.copy(wide[r][:, half_columns(0)], banks[r][0][:])
        for r in range(PACK):
            nc.vector.tensor_copy(wide[r][:, half_columns(1)], banks[r][1][:])

        minus = [sb.tile([P, J], F32, name="minus%d" % r) for r in range(PACK)]
        diff = [sb.tile([P, J], F32, name="diff%d" % r) for r in range(PACK)]
        table = [sb.tile([P, J], F32, name="table%d" % r) for r in range(PACK)]
        y = [sb.tile([P, PACK, BANK], F32, name="y%d" % h) for h in range(2)]

        def look_up_minus(r):
            nc.scalar.activation(minus[r][:], wide[r][:].indirect(list3[:]), ACT.Copy)

        def look_up_diff(r):
            nc.vector.tensor_tensor(diff[r][:], wide[r][:].indirect(list2[:]), minus[r][:], ALU.subtract)

        def squash(r):
            nc.scalar.activation(table[r][:], diff[r][:], ACT.Tanh)

        def places(r, first, count):
            return placed[r][:].indirect(list4[:, first // PER_COLUMN : (first + count) // PER_COLUMN])

        def place_by_vector(r, first, count):
            nc.vector.tensor_copy(places(r, first, count), table[r][:, first : first + count])

        def place_by_scalar(r, first, count):
            nc.scalar.activation(places(r, first, count), table[r][:, first : first + count], ACT.Copy)

        def combine(r, first, width):
            cols = slice(first, first + width)
            nc.vector.scalar_tensor_tensor(
                y[first // BANK][:, r, first % BANK : first % BANK + width],
                old_sb[r][:, cols],
                fade_sb[:, r : r + 1],
                placed[r][:, cols],
                ALU.mult,
                ALU.add,
            )

        def store(r, h):
            nc.sync.dma_start(out_v[:, r, half_columns(h)], y[h][:, r, :])

        look_up_minus(0)
        nc.scalar.copy(wide[LAST][:, half_columns(0)], banks[LAST][0][:])
        for r in range(1, PACK):
            look_up_minus(r)
        for r in range(PACK):
            look_up_diff(r)

        squash(0)
        squash(1)
        place_by_vector(0, 0, J)
        place_by_scalar(1, 0, HALF_LIST)
        squash(2)
        squash(LAST)
        place_by_vector(LAST, 0, VECTOR_SHARE)
        place_by_scalar(2, 0, HALF_LIST)
        place_by_scalar(1, HALF_LIST, HALF_LIST)
        place_by_scalar(2, HALF_LIST, HALF_LIST)
        place_by_scalar(LAST, VECTOR_SHARE, J - VECTOR_SHARE)

        faded = sb.tile([P, M], F32, name="wide%d" % LAST)
        nc.gpsimd.tensor_scalar(faded[:], old_sb[0][:], fade_sb[:, 0:1], 0.0, ALU.mult, ALU.add)
        for h in range(2):
            cols = half_columns(h)
            nc.gpsimd.tensor_tensor(y[h][:, 0, :], faded[:, cols], placed[0][:, cols], ALU.add)
            store(0, h)
        for r in range(1, LAST):
            for h in range(2):
                combine(r, h * BANK, BANK)
                store(r, h)

        y_codes = sb.tile([P, M], U32, name="y_codes", align_bytes=64)
        y_scales = sb.tile([P, M], U8, name="y_scales", align_bytes=64)
        y_grouped = [sb.tile([P, CHUNK, PACK], BF16, name="y_grouped%d" % c, align_bytes=64) for c in range(CHUNKS)]
        words_v = out_1[0].rearrange("p c r -> p (c r)").bitcast(I32)
        for h in range(2):
            combine(LAST, h * BANK, CHUNK)
            combine(LAST, h * BANK + CHUNK, CHUNK)
            store(LAST, h)
        for c in range(CHUNKS):
            copy = nc.scalar.copy if c < CHUNKS // 2 else nc.vector.tensor_copy
            interleave(copy, y_grouped[c][:], y[c // 2][:, :, chunk_columns(c % 2)])
        for c in (0, 2, 3, 1):
            cols = chunk_columns(c)
            nc.vector.quantize_mx(
                out=y_codes[:, cols].bitcast(FP8X4),
                scales=y_scales[:, cols],
                in_=y_grouped[c][:].rearrange("p c r -> p (c r)"),
            )
            nc.sync.dma_start(words_v[:, cols], y_codes[:, cols].bitcast(I32))
        for k in range(SCALE_ROWS):
            (nc.scalar if k % 2 else nc.sync).dma_start(
                out_2[0, k:BLOCKS:SCALE_ROWS, :].bitcast(I32), y_scales[k:P:QUADRANT, :].bitcast(I32)
            )
